import numpy as np
import ml_dtypes


def mxq(x, axis, fmt="e4m3"):
    dtype, down = {"e4m3": (ml_dtypes.float8_e4m3fn, 7), "e5m2": (ml_dtypes.float8_e5m2, 14)}[fmt]
    v = np.moveaxis(np.asarray(x, np.float32).astype(ml_dtypes.bfloat16).astype(np.float64), axis, -1)
    blocks = v.reshape(v.shape[:-1] + (-1, 32))
    amax = np.abs(blocks).max(-1, keepdims=True)
    byte = np.maximum(np.where(amax > 0, np.frexp(amax)[1] - 1 + 127, 0) - down, 1)
    scale = np.exp2(byte - 127.0)
    codes = (blocks / scale).astype(np.float32).astype(dtype).astype(np.float64)
    return np.moveaxis((codes * scale).reshape(v.shape), -1, axis)


WIDE = False


def mx_kscale(k):
    if not WIDE:
        return np.ones(k)
    levels = np.array([10, -10, 5, -5, 0])
    if k % 512:
        return np.exp2(np.random.permutation(np.resize(levels, k // 32))).repeat(32)
    a = np.empty((k // 512, 16))
    for p in range(k // 512):
        a[p, :8] = np.random.permutation(np.resize(levels, 8))
        for g in range(8):
            far = levels[np.abs(levels - a[p, g]) >= 10]
            a[p, g + 8] = far[np.random.randint(len(far))]
    return np.exp2(a.ravel()).repeat(32)


def f64(x):
    return np.asarray(x).astype(np.float64)


def striped(idx):
    return np.tile(np.asarray(idx).reshape(-1, 16).T, (8, 1)).astype(np.uint16)


def unstriped(offs):
    return offs[:16].T.reshape(-1).astype(np.int64)


E2M1 = np.array([0.0, 0.5, 1.0, 1.5, 2.0, 3.0, 4.0, 6.0, -0.0, -0.5, -1.0, -1.5, -2.0, -3.0, -4.0, -6.0])


def pack_weight(w, fmt):
    k, n = w.shape
    w = f64(np.asarray(w, np.float32).astype(ml_dtypes.bfloat16)).reshape(k // 32, 32, n)
    amax = np.abs(w).max(1)
    if fmt == "e4m3":
        byte = np.frexp(amax)[1] - 1 + 127 - 7
    else:
        mant, ex = np.frexp(amax / 6.0)
        byte = np.where(mant > 0.5, ex, ex - 1) + 127
    byte = np.clip(np.where(amax > 0, byte, 1), 1, 254)
    scaled = (w * np.exp2(127.0 - byte)[:, None, :]).reshape(k, n).astype(np.float32)
    by_word = np.ascontiguousarray(scaled.reshape(k // 512, 128, 4, n).transpose(0, 1, 3, 2))
    if fmt == "e4m3":
        words = by_word.astype(ml_dtypes.float8_e4m3fn).view(np.uint8)
    else:
        c = by_word.astype(ml_dtypes.float4_e2m1fn).view(np.uint8) & 0xF
        words = (c[..., 0::2] | (c[..., 1::2] << 4)).reshape(k // 512, 128, 2 * n)
    return np.ascontiguousarray(words), np.ascontiguousarray(byte.astype(np.uint8).reshape(k // 512, 16, n))


def unpack_weight(words, scales, fmt):
    g, _, n = scales.shape
    words = np.ascontiguousarray(words).reshape(g, 128, n, -1)
    if fmt == "e4m3":
        vals = words.view(ml_dtypes.float8_e4m3fn).astype(np.float64)
    else:
        nib = np.empty((g, 128, n, 4), np.uint8)
        nib[..., 0::2] = words & 0xF
        nib[..., 1::2] = words >> 4
        vals = E2M1[nib]
    vals = vals * np.repeat(np.exp2(scales.astype(np.float64) - 127.0), 8, axis=1)[..., None]
    return vals.transpose(0, 1, 3, 2).reshape(g * 512, n)


def bf(x):
    return np.asarray(x, np.float32).astype(ml_dtypes.bfloat16)


def planes(Y):
    r, m = Y.shape
    b = f64(bf(Y)).reshape(r // 32, 32, m)
    amax = np.abs(b).max(1)
    byte = np.clip(np.where(amax > 0, np.frexp(amax)[1] - 1 + 127 - 7, 1), 1, 254)
    codes = (b * np.exp2(127.0 - byte)[:, None, :]).reshape(r, m).astype(np.float32).astype(ml_dtypes.float8_e4m3fn).view(np.uint8)
    words = codes.reshape(r // 512, 128, 4, m).transpose(0, 1, 3, 2)
    return np.ascontiguousarray(words), np.ascontiguousarray(byte.astype(np.uint8).reshape(r // 512, 16, m))


D, T, I, Q, E = 512, 2048, 512, 256, 512


def setup_inputs():
    n = np.random.standard_normal
    idx = np.random.permutation(T)[:I]
    fd = mx_kscale(D)
    fi = mx_kscale(I)
    ti = np.ones(T)
    ti[idx] = fi
    keysp = pack_weight(n((D, T)) / fd[:, None], "e2m1")
    return {
        "query": (n((D, Q)) * 0.25 / np.sqrt(D) * fd[:, None]).astype(np.float32),
        "avoid": (n((D, Q)) * 1.0 / np.sqrt(D) * fd[:, None]).astype(np.float32),
        "keys_words": keysp[0],
        "keys_scales": keysp[1],
        "aver": (np.random.uniform(0.5, 1.5, (Q, 1))).astype(np.float32),
        "size": (np.random.uniform(0.5, 2.0, (1, I)) * fi).astype(np.float32),
        "vals": (n((E, T)) / ti).astype(np.float32),
        "offs": striped(idx),
    }


def reference(query, avoid, keys_words, keys_scales, aver, size, vals, offs):
    idx = unstriped(offs)
    keysu = unpack_weight(keys_words, keys_scales, "e2m1")
    queryq = mxq(f64(query), 0, "e4m3")
    keysidxg = keysu[:, idx]
    a = queryq.T @ keysidxg
    avoidq = mxq(f64(avoid), 0, "e4m3")
    b = avoidq.T @ keysidxg
    s = a - np.maximum(b, 0.0) * f64(aver)
    p = np.exp(s - np.max(s, axis=1, keepdims=True))
    w = p * f64(size) / np.sum(p, axis=1, keepdims=True)
    wt = w.T
    vt = f64(vals)[:, idx].T
    vtq = mxq(vt, 0, "e4m3")
    wtq = mxq(wt, 0, "e4m3")
    o = vtq.T @ wtq
    words, scales = planes(o)
    return o, words, scales

@@ -1,0 +1,200 @@
+from contextlib import ExitStack
+
+import concourse.mybir as mybir
+from concourse.masks import make_identity
+
+D, T, I, Q, E = 512, 2048, 512, 256, 512
+P = 128
+PACK = 4
+QT = Q // P
+FLOPS = 2 * D * Q * I * 2 + 2 * I * E * Q
+
+F32 = mybir.dt.float32
+BF16 = mybir.dt.bfloat16
+I32 = mybir.dt.int32
+U32 = mybir.dt.uint32
+U16 = mybir.dt.uint16
+U8 = mybir.dt.uint8
+FP8X4 = mybir.dt.float8_e4m3fn_x4
+FP4X4 = mybir.dt.float4_e2m1fn_x4
+ALU = mybir.AluOpType
+ACT = mybir.ActivationFunctionType
+AXIS = mybir.AxisListType
+
+
+def tile_attend_antiquery_pl_kernel(tc, query, avoid, keys_words, keys_scales, aver, size, vals, offs, out_0, out_1, out_2):
+    nc = tc.nc
+    with ExitStack() as ctx:
+        sb = ctx.enter_context(tc.tile_pool(name="sb", bufs=1))
+        ps = ctx.enter_context(tc.psum_pool(name="ps", bufs=1))
+
+        def tile(shape, dtype, name, tag=None):
+            return sb.tile(shape, dtype, name=name, tag=tag or name, align_bytes=64)
+
+        def bank(shape, tag, name):
+            return ps.tile(shape, F32, tag=tag, name=name)
+
+        offsets = sb.tile([P, I // 16], U16, name="offsets")
+        nc.sync.dma_start(offsets[:], offs)
+
+        pool_scales = tile([P, T], U8, "pool_scales")
+        nc.gpsimd.memset(pool_scales[:].bitcast(I32), 0)
+        pool_words = tile([P, T], U16, "pool_words")
+        nc.sync.dma_start(pool_words[:].bitcast(I32), keys_words[0].bitcast(I32))
+        for g in range(4):
+            nc.sync.dma_start(pool_scales[32 * g : 32 * g + 4, :].bitcast(I32), keys_scales[0, 4 * g : 4 * g + 4, :].bitcast(I32))
+        avoid_raw = tile([P, PACK, Q], F32, "avoid_raw")
+        nc.sync.dma_start(avoid_raw[:], avoid.rearrange("(p j) q -> p j q", j=PACK))
+        query_raw = tile([P, PACK, Q], F32, "query_raw")
+        nc.sync.dma_start(query_raw[:], query.rearrange("(p j) q -> p j q", j=PACK))
+        vals_rows = vals.rearrange("(p j) t -> j p t", j=PACK)
+        pool_vals = []
+
+        def load_vals(j, tag):
+            pv = tile([P, T], F32, f"pool_vals{j}", tag)
+            nc.sync.dma_start(pv[:], vals_rows[j])
+            pool_vals.append(pv)
+
+        load_vals(0, None)
+        aver_cols = tile([P, QT], F32, "aver_cols")
+        with nc.allow_non_contiguous_dma(reason="one value a partition"):
+            nc.sync.dma_start(aver_cols[:], aver.rearrange("(h p) o -> p (h o)", p=P))
+        size_cols = tile([P, PACK], F32, "size_cols")
+        nc.sync.dma_start(size_cols[:], size.rearrange("o (p j) -> p (o j)", j=PACK))
+        for j in range(1, PACK):
+            load_vals(j, None)
+        ident = tile([P, P], F32, "ident")
+        make_identity(nc, ident[:])
+
+        warm = tile([P, 1], F32, "warm")
+        nc.scalar.activation(warm[:], ident[:, 0:1], ACT.Exp)
+
+        def interleave(engine_copy, dst, src):
+            engine_copy(dst.rearrange("p (c i) t -> p c t i", i=4), src.rearrange("p t (c i) -> p c t i", i=4))
+
+        def quantize(codes, scales, grouped):
+            nc.vector.quantize_mx(out=codes.bitcast(FP8X4), scales=scales, in_=grouped)
+
+        avoid_bf = tile([P, Q, PACK], BF16, "avoid_bf")
+        interleave(nc.scalar.copy, avoid_bf[:], avoid_raw[:])
+        key_words = tile([P, I], U16, "key_words")
+        nc.vector.tensor_copy(key_words[:], pool_words[:].indirect(offsets[:]))
+        key_scales = tile([P, I], U8, "key_scales")
+        nc.vector.tensor_copy(key_scales[:], pool_scales[:].indirect(offsets[:]))
+        query_bf = [tile([P, P, PACK], BF16, f"query_bf{h}") for h in range(QT)]
+        interleave(nc.scalar.copy, query_bf[0][:], query_raw[:, :, 0:P])
+        interleave(nc.vector.tensor_copy, query_bf[1][:], query_raw[:, :, P : 2 * P])
+        avoid_codes = tile([P, Q], U32, "avoid_codes")
+        avoid_scales = tile([P, Q], U8, "avoid_scales")
+        quantize(avoid_codes[:], avoid_scales[:], avoid_bf[:].rearrange("p q t -> p (q t)"))
+
+
+        def scores(dst, codes, scales):
+            nc.tensor.matmul_mx(out=dst, lhsT=codes.bitcast(FP8X4), lhsT_scale=scales,
+                                rhs=key_words[:].bitcast(FP4X4), rhs_scale=key_scales[:], start=True, stop=True)
+
+        a_banks, b_banks = [], []
+        for h in range(QT):
+            bb = bank([P, I], f"b{h}", f"b_bank{h}")
+            scores(bb[:], avoid_codes[:, h * P : (h + 1) * P], avoid_scales[:, h * P : (h + 1) * P])
+            b_banks.append(bb)
+            qc = tile([P, P], U32, f"query_codes{h}")
+            qs = tile([P, P], U8, f"query_scales{h}")
+            quantize(qc[:], qs[:], query_bf[h][:].rearrange("p q t -> p (q t)"))
+            ab = bank([P, I], f"a{h}", f"a_bank{h}")
+            scores(ab[:], qc[:], qs[:])
+            a_banks.append(ab)
+
+        size_bank = bank([P, PACK, P], "size", "size_bank")
+        for j in range(PACK):
+            nc.tensor.transpose(size_bank[:, j, :], size_cols[:, j : j + 1].to_broadcast([P, P]), ident[:])
+
+        neg_s, neg_max, probs = [], [], []
+        for h in range(QT):
+            pos = tile([P, I], F32, f"pos{h}")
+            nc.scalar.activation(pos[:], b_banks[h][:], ACT.Relu)
+            ns = tile([P, I], F32, f"neg_s{h}")
+            nc.vector.scalar_tensor_tensor(ns[:], pos[:], aver_cols[:, h : h + 1], a_banks[h][:], ALU.mult, ALU.subtract)
+            neg_s.append(ns)
+        totals = tile([P, QT], F32, "totals")
+        for h in range(QT):
+            nm = tile([P, 1], F32, f"neg_max{h}")
+            nc.vector.tensor_reduce(nm[:], neg_s[h][:], AXIS.X, ALU.min)
+            prob = tile([P, I], F32, f"prob{h}")
+            nc.scalar.activation(prob[:], neg_s[h][:], ACT.Exp, bias=nm[:], scale=-1.0, accum_out=totals[:, h : h + 1])
+            probs.append(prob)
+
+        def turn(src_bf, tag, name, grouped):
+            words = src_bf[:].bitcast(F32)
+            turned = bank([P, 2, P], tag, name + "_bank")
+            for u in range(2):
+                nc.tensor.transpose(turned[:, u, :], words[:, u : 2 * P : 2], ident[:])
+            nc.scalar.copy(grouped.bitcast(F32).rearrange("p (r u) -> p r u", u=2), turned[:].rearrange("p u r -> p r u"))
+
+        def gather_vals(j):
+            picked = tile([P, I], BF16, f"picked{j}")
+            nc.vector.tensor_copy(picked[:], pool_vals[j][:].indirect(offsets[:]))
+            grouped = tile([P, P * PACK], BF16, f"vt{j}_grouped")
+            turn(picked, ("b0", "b1")[j % 2], f"vt{j}", grouped[:])
+            return grouped
+
+        def weights(h):
+            w = tile([P, I], BF16, f"w{h}")
+            nc.vector.scalar_tensor_tensor(w[:].rearrange("p (n j) -> p n j", j=PACK), probs[h][:].rearrange("p (n j) -> p n j", j=PACK),
+                                           inv[:, h : h + 1], size_bank[:].rearrange("p j n -> p n j"), ALU.mult, ALU.mult)
+            turn(w, f"w{h}", f"wt{h}", wt_grouped[:, h * I : (h + 1) * I])
+
+        def quantize_tile(grouped, name):
+            codes = tile([P, P], U32, name + "_codes")
+            scales = tile([P, P], U8, name + "_scales")
+            quantize(codes[:], scales[:], grouped[:])
+            return codes, scales
+
+        o_banks = [bank([P, PACK, P], f"a{h}", f"o_bank{h}") for h in range(QT)]
+        result = tile([P, PACK, Q], F32, "result")
+        out_rows = out_0.rearrange("(p j) q -> p j q", j=PACK)
+
+        def product(j, vt):
+            for h in range(QT):
+                nc.tensor.matmul_mx(out=o_banks[h][:, j, :], lhsT=vt[0][:].bitcast(FP8X4), lhsT_scale=vt[1][:],
+                                    rhs=wt_codes[:, h * P : (h + 1) * P].bitcast(FP8X4), rhs_scale=wt_scales[:, h * P : (h + 1) * P], start=True, stop=True)
+
+        def unload(rows):
+            for h in range(QT):
+                nc.scalar.copy(result[:, rows, h * P : (h + 1) * P], o_banks[h][:, rows, :])
+            nc.sync.dma_start(out_rows[:, rows, :], result[:, rows, :])
+
+        vg0 = gather_vals(0)
+        inv = tile([P, QT], F32, "inv")
+        nc.vector.reciprocal(inv[:], totals[:])
+        wt_grouped = tile([P, QT * I], BF16, "wt_grouped")
+        for h in range(QT):
+            weights(h)
+        vg1 = gather_vals(1)
+        vt0 = quantize_tile(vg0, "vt0")
+        wt_codes = tile([P, Q], U32, "wt_codes")
+        wt_scales = tile([P, Q], U8, "wt_scales")
+        quantize(wt_codes[:], wt_scales[:], wt_grouped[:])
+        product(0, vt0)
+        vg2 = gather_vals(2)
+        product(1, quantize_tile(vg1, "vt1"))
+        unload(slice(0, 2))
+        vg3 = gather_vals(3)
+        product(2, quantize_tile(vg2, "vt2"))
+        unload(slice(2, 3))
+        product(3, quantize_tile(vg3, "vt3"))
+
+        out_codes = tile([P, Q], U32, "out_codes")
+        out_scales = tile([P, Q], U8, "out_scales")
+        result_bf = [tile([P, P, PACK], BF16, f"result_bf{h}") for h in range(QT)]
+        nc.vector.tensor_copy(result_bf[0][:], o_banks[0][:].rearrange("p j q -> p q j"))
+        nc.scalar.copy(result_bf[1][:], o_banks[1][:].rearrange("p j q -> p q j"))
+        for h in range(QT):
+            quantize(out_codes[:, h * P : (h + 1) * P], out_scales[:, h * P : (h + 1) * P], result_bf[h][:].rearrange("p q j -> p (q j)"))
+        for h in (1, 0):
+            nc.scalar.copy(result[:, 3, h * P : (h + 1) * P], o_banks[h][:, 3, :])
+        nc.sync.dma_start(out_1[0].rearrange("p q r -> p (q r)").bitcast(I32), out_codes[:].bitcast(I32))
+        for g in range(4):
+            queue = (nc.sync, nc.scalar)[g % 2]
+            queue.dma_start(out_2[0, 4 * g : 4 * g + 4, :].bitcast(I32), out_scales[32 * g : 32 * g + 4, :].bitcast(I32))
+        nc.sync.dma_start(out_rows[:, 3, :], result[:, 3, :])

@@ -6,7 +6,8 @@ from concourse.masks import make_identity
 D, T, I, Q, E = 512, 2048, 512, 256, 512
 P = 128
 PACK = 4
-QT = Q // P
+HALVES = Q // P
+QUADRANTS = 4
 FLOPS = 2 * D * Q * I * 2 + 2 * I * E * Q
 
 F32 = mybir.dt.float32
@@ -25,176 +26,184 @@ AXIS = mybir.AxisListType
 def tile_attend_antiquery_pl_kernel(tc, query, avoid, keys_words, keys_scales, aver, size, vals, offs, out_0, out_1, out_2):
     nc = tc.nc
     with ExitStack() as ctx:
-        sb = ctx.enter_context(tc.tile_pool(name="sb", bufs=1))
-        ps = ctx.enter_context(tc.psum_pool(name="ps", bufs=1))
+        sbuf = ctx.enter_context(tc.tile_pool(name="sbuf", bufs=1))
+        psum = ctx.enter_context(tc.psum_pool(name="psum", bufs=1))
 
-        def tile(shape, dtype, name, tag=None):
-            return sb.tile(shape, dtype, name=name, tag=tag or name, align_bytes=64)
+        def tile(shape, dtype, name, reuse=None):
+            return sbuf.tile(shape, dtype, name=name, tag=reuse or name, align_bytes=64)
 
         def bank(shape, tag, name):
-            return ps.tile(shape, F32, tag=tag, name=name)
+            return psum.tile(shape, F32, tag=tag, name=name)
 
-        offsets = sb.tile([P, I // 16], U16, name="offsets")
+        def half(h):
+            return slice(h * P, (h + 1) * P)
+
+        def scale_rows(g):
+            return slice(32 * g, 32 * g + 4)
+
+        offsets = sbuf.tile([P, I // 16], U16, name="offsets")
         nc.sync.dma_start(offsets[:], offs)
 
         pool_scales = tile([P, T], U8, "pool_scales")
         nc.gpsimd.memset(pool_scales[:].bitcast(I32), 0)
         pool_words = tile([P, T], U16, "pool_words")
         nc.sync.dma_start(pool_words[:].bitcast(I32), keys_words[0].bitcast(I32))
-        for g in range(4):
-            nc.sync.dma_start(pool_scales[32 * g : 32 * g + 4, :].bitcast(I32), keys_scales[0, 4 * g : 4 * g + 4, :].bitcast(I32))
+        for g in range(QUADRANTS):
+            nc.sync.dma_start(pool_scales[scale_rows(g), :].bitcast(I32), keys_scales[0, 4 * g : 4 * g + 4, :].bitcast(I32))
         avoid_raw = tile([P, PACK, Q], F32, "avoid_raw")
-        nc.sync.dma_start(avoid_raw[:], avoid.rearrange("(p j) q -> p j q", j=PACK))
+        nc.sync.dma_start(avoid_raw[:], avoid.rearrange("(p t) q -> p t q", t=PACK))
         query_raw = tile([P, PACK, Q], F32, "query_raw")
-        nc.sync.dma_start(query_raw[:], query.rearrange("(p j) q -> p j q", j=PACK))
-        vals_rows = vals.rearrange("(p j) t -> j p t", j=PACK)
+        nc.sync.dma_start(query_raw[:], query.rearrange("(p t) q -> p t q", t=PACK))
+
+        vals_rows = vals.rearrange("(p j) c -> j p c", j=PACK)
         pool_vals = []
 
-        def load_vals(j, tag):
-            pv = tile([P, T], F32, f"pool_vals{j}", tag)
-            nc.sync.dma_start(pv[:], vals_rows[j])
-            pool_vals.append(pv)
+        def load_vals(j):
+            window = tile([P, T], F32, f"pool_vals{j}")
+            nc.sync.dma_start(window[:], vals_rows[j])
+            pool_vals.append(window)
 
-        load_vals(0, None)
-        aver_cols = tile([P, QT], F32, "aver_cols")
+        load_vals(0)
+        aver_cols = tile([P, HALVES], F32, "aver_cols")
         with nc.allow_non_contiguous_dma(reason="one value a partition"):
             nc.sync.dma_start(aver_cols[:], aver.rearrange("(h p) o -> p (h o)", p=P))
         size_cols = tile([P, PACK], F32, "size_cols")
-        nc.sync.dma_start(size_cols[:], size.rearrange("o (p j) -> p (o j)", j=PACK))
+        nc.sync.dma_start(size_cols[:], size.rearrange("o (p t) -> p (o t)", t=PACK))
         for j in range(1, PACK):
-            load_vals(j, None)
+            load_vals(j)
         ident = tile([P, P], F32, "ident")
         make_identity(nc, ident[:])
 
-        warm = tile([P, 1], F32, "warm")
-        nc.scalar.activation(warm[:], ident[:, 0:1], ACT.Exp)
+        def group(engine_copy, grouped, raw):
+            engine_copy(grouped.rearrange("p (c n) t -> p c t n", n=4), raw.rearrange("p t (c n) -> p c t n", n=4))
 
-        def interleave(engine_copy, dst, src):
-            engine_copy(dst.rearrange("p (c i) t -> p c t i", i=4), src.rearrange("p t (c i) -> p c t i", i=4))
+        def activation_copy(dst, src):
+            nc.scalar.activation(dst, src, ACT.Copy)
 
         def quantize(codes, scales, grouped):
             nc.vector.quantize_mx(out=codes.bitcast(FP8X4), scales=scales, in_=grouped)
 
-        avoid_bf = tile([P, Q, PACK], BF16, "avoid_bf")
-        interleave(nc.scalar.copy, avoid_bf[:], avoid_raw[:])
+        avoid_grouped = tile([P, Q, PACK], BF16, "avoid_grouped")
+        group(activation_copy, avoid_grouped[:], avoid_raw[:])
         key_words = tile([P, I], U16, "key_words")
         nc.vector.tensor_copy(key_words[:], pool_words[:].indirect(offsets[:]))
         key_scales = tile([P, I], U8, "key_scales")
         nc.vector.tensor_copy(key_scales[:], pool_scales[:].indirect(offsets[:]))
-        query_bf = [tile([P, P, PACK], BF16, f"query_bf{h}") for h in range(QT)]
-        interleave(nc.scalar.copy, query_bf[0][:], query_raw[:, :, 0:P])
-        interleave(nc.vector.tensor_copy, query_bf[1][:], query_raw[:, :, P : 2 * P])
+        query_grouped = [tile([P, P, PACK], BF16, f"query_grouped{h}") for h in range(HALVES)]
+        group(nc.scalar.copy, query_grouped[0][:], query_raw[:, :, half(0)])
+        group(nc.vector.tensor_copy, query_grouped[1][:], query_raw[:, :, half(1)])
         avoid_codes = tile([P, Q], U32, "avoid_codes")
         avoid_scales = tile([P, Q], U8, "avoid_scales")
-        quantize(avoid_codes[:], avoid_scales[:], avoid_bf[:].rearrange("p q t -> p (q t)"))
-
+        quantize(avoid_codes[:], avoid_scales[:], avoid_grouped[:].rearrange("p q t -> p (q t)"))
 
         def scores(dst, codes, scales):
             nc.tensor.matmul_mx(out=dst, lhsT=codes.bitcast(FP8X4), lhsT_scale=scales,
                                 rhs=key_words[:].bitcast(FP4X4), rhs_scale=key_scales[:], start=True, stop=True)
 
         a_banks, b_banks = [], []
-        for h in range(QT):
-            bb = bank([P, I], f"b{h}", f"b_bank{h}")
-            scores(bb[:], avoid_codes[:, h * P : (h + 1) * P], avoid_scales[:, h * P : (h + 1) * P])
-            b_banks.append(bb)
-            qc = tile([P, P], U32, f"query_codes{h}")
-            qs = tile([P, P], U8, f"query_scales{h}")
-            quantize(qc[:], qs[:], query_bf[h][:].rearrange("p q t -> p (q t)"))
-            ab = bank([P, I], f"a{h}", f"a_bank{h}")
-            scores(ab[:], qc[:], qs[:])
-            a_banks.append(ab)
+        for h in range(HALVES):
+            b_bank = bank([P, I], f"b{h}", f"b_bank{h}")
+            scores(b_bank[:], avoid_codes[:, half(h)], avoid_scales[:, half(h)])
+            b_banks.append(b_bank)
+            query_codes = tile([P, P], U32, f"query_codes{h}")
+            query_scales = tile([P, P], U8, f"query_scales{h}")
+            quantize(query_codes[:], query_scales[:], query_grouped[h][:].rearrange("p q t -> p (q t)"))
+            a_bank = bank([P, I], f"a{h}", f"a_bank{h}")
+            scores(a_bank[:], query_codes[:], query_scales[:])
+            a_banks.append(a_bank)
 
         size_bank = bank([P, PACK, P], "size", "size_bank")
-        for j in range(PACK):
-            nc.tensor.transpose(size_bank[:, j, :], size_cols[:, j : j + 1].to_broadcast([P, P]), ident[:])
+        for t in range(PACK):
+            nc.tensor.transpose(size_bank[:, t, :], size_cols[:, t : t + 1].to_broadcast([P, P]), ident[:])
 
-        neg_s, neg_max, probs = [], [], []
-        for h in range(QT):
-            pos = tile([P, I], F32, f"pos{h}")
-            nc.scalar.activation(pos[:], b_banks[h][:], ACT.Relu)
-            ns = tile([P, I], F32, f"neg_s{h}")
-            nc.vector.scalar_tensor_tensor(ns[:], pos[:], aver_cols[:, h : h + 1], a_banks[h][:], ALU.mult, ALU.subtract)
-            neg_s.append(ns)
-        totals = tile([P, QT], F32, "totals")
-        for h in range(QT):
-            nm = tile([P, 1], F32, f"neg_max{h}")
-            nc.vector.tensor_reduce(nm[:], neg_s[h][:], AXIS.X, ALU.min)
+        neg_scores, probs = [], []
+        for h in range(HALVES):
+            positive = tile([P, I], F32, f"positive{h}")
+            nc.scalar.activation(positive[:], b_banks[h][:], ACT.Relu)
+            neg_s = tile([P, I], F32, f"neg_s{h}")
+            nc.vector.scalar_tensor_tensor(neg_s[:], positive[:], aver_cols[:, h : h + 1], a_banks[h][:], ALU.mult, ALU.subtract)
+            neg_scores.append(neg_s)
+        totals = tile([P, HALVES], F32, "totals")
+        for h in range(HALVES):
+            neg_max = tile([P, 1], F32, f"neg_max{h}")
+            nc.vector.tensor_reduce(neg_max[:], neg_scores[h][:], AXIS.X, ALU.min)
             prob = tile([P, I], F32, f"prob{h}")
-            nc.scalar.activation(prob[:], neg_s[h][:], ACT.Exp, bias=nm[:], scale=-1.0, accum_out=totals[:, h : h + 1])
+            nc.scalar.activation(prob[:], neg_scores[h][:], ACT.Exp, bias=neg_max[:], scale=-1.0, accum_out=totals[:, h : h + 1])
             probs.append(prob)
 
-        def turn(src_bf, tag, name, grouped):
-            words = src_bf[:].bitcast(F32)
+        def turn(rows, tag, name, grouped):
+            pairs = rows[:].bitcast(F32)
             turned = bank([P, 2, P], tag, name + "_bank")
             for u in range(2):
-                nc.tensor.transpose(turned[:, u, :], words[:, u : 2 * P : 2], ident[:])
+                nc.tensor.transpose(turned[:, u, :], pairs[:, u : 2 * P : 2], ident[:])
             nc.scalar.copy(grouped.bitcast(F32).rearrange("p (r u) -> p r u", u=2), turned[:].rearrange("p u r -> p r u"))
 
         def gather_vals(j):
             picked = tile([P, I], BF16, f"picked{j}")
             nc.vector.tensor_copy(picked[:], pool_vals[j][:].indirect(offsets[:]))
             grouped = tile([P, P * PACK], BF16, f"vt{j}_grouped")
-            turn(picked, ("b0", "b1")[j % 2], f"vt{j}", grouped[:])
+            turn(picked, f"b{j % 2}", f"vt{j}", grouped[:])
             return grouped
 
         def weights(h):
             w = tile([P, I], BF16, f"w{h}")
-            nc.vector.scalar_tensor_tensor(w[:].rearrange("p (n j) -> p n j", j=PACK), probs[h][:].rearrange("p (n j) -> p n j", j=PACK),
-                                           inv[:, h : h + 1], size_bank[:].rearrange("p j n -> p n j"), ALU.mult, ALU.mult)
+            nc.vector.scalar_tensor_tensor(w[:].rearrange("p (n t) -> p n t", t=PACK), probs[h][:].rearrange("p (n t) -> p n t", t=PACK),
+                                           inverses[:, h : h + 1], size_bank[:].rearrange("p t n -> p n t"), ALU.mult, ALU.mult)
             turn(w, f"w{h}", f"wt{h}", wt_grouped[:, h * I : (h + 1) * I])
 
-        def quantize_tile(grouped, name):
-            codes = tile([P, P], U32, name + "_codes")
-            scales = tile([P, P], U8, name + "_scales")
+        def quantize_vals(grouped, j, reuse=None):
+            codes = tile([P, P], U32, f"vt{j}_codes", reuse)
+            scales = tile([P, P], U8, f"vt{j}_scales")
             quantize(codes[:], scales[:], grouped[:])
             return codes, scales
 
-        o_banks = [bank([P, PACK, P], f"a{h}", f"o_bank{h}") for h in range(QT)]
+        o_banks = [bank([P, PACK, P], f"a{h}", f"o_bank{h}") for h in range(HALVES)]
         result = tile([P, PACK, Q], F32, "result")
         out_rows = out_0.rearrange("(p j) q -> p j q", j=PACK)
 
         def product(j, vt):
-            for h in range(QT):
-                nc.tensor.matmul_mx(out=o_banks[h][:, j, :], lhsT=vt[0][:].bitcast(FP8X4), lhsT_scale=vt[1][:],
-                                    rhs=wt_codes[:, h * P : (h + 1) * P].bitcast(FP8X4), rhs_scale=wt_scales[:, h * P : (h + 1) * P], start=True, stop=True)
+            codes, scales = vt
+            for h in range(HALVES):
+                nc.tensor.matmul_mx(out=o_banks[h][:, j, :], lhsT=codes[:].bitcast(FP8X4), lhsT_scale=scales[:],
+                                    rhs=wt_codes[:, half(h)].bitcast(FP8X4), rhs_scale=wt_scales[:, half(h)], start=True, stop=True)
 
-        def unload(rows):
-            for h in range(QT):
-                nc.scalar.copy(result[:, rows, h * P : (h + 1) * P], o_banks[h][:, rows, :])
-            nc.sync.dma_start(out_rows[:, rows, :], result[:, rows, :])
+        def unload(js, copies):
+            for h in range(HALVES):
+                copies[h](result[:, js, half(h)], o_banks[h][:, js, :])
+            nc.sync.dma_start(out_rows[:, js, :], result[:, js, :])
 
-        vg0 = gather_vals(0)
-        inv = tile([P, QT], F32, "inv")
-        nc.vector.reciprocal(inv[:], totals[:])
-        wt_grouped = tile([P, QT * I], BF16, "wt_grouped")
-        for h in range(QT):
+        vt0_grouped = gather_vals(0)
+        inverses = tile([P, HALVES], F32, "inverses")
+        nc.vector.reciprocal(inverses[:], totals[:])
+        wt_grouped = tile([P, HALVES * I], BF16, "wt_grouped")
+        for h in range(HALVES):
             weights(h)
-        vg1 = gather_vals(1)
-        vt0 = quantize_tile(vg0, "vt0")
+        vt1_grouped = gather_vals(1)
+        vt0 = quantize_vals(vt0_grouped, 0)
         wt_codes = tile([P, Q], U32, "wt_codes")
         wt_scales = tile([P, Q], U8, "wt_scales")
         quantize(wt_codes[:], wt_scales[:], wt_grouped[:])
         product(0, vt0)
-        vg2 = gather_vals(2)
-        product(1, quantize_tile(vg1, "vt1"))
-        unload(slice(0, 2))
-        vg3 = gather_vals(3)
-        product(2, quantize_tile(vg2, "vt2"))
-        unload(slice(2, 3))
-        product(3, quantize_tile(vg3, "vt3"))
+        vt2_grouped = gather_vals(2)
+        product(1, quantize_vals(vt1_grouped, 1))
+        unload(slice(0, 2), (nc.scalar.copy, nc.scalar.copy))
+        vt3_grouped = gather_vals(3)
+        product(2, quantize_vals(vt2_grouped, 2, reuse="pool_vals3"))
+        unload(slice(2, 3), (nc.vector.tensor_copy, nc.scalar.copy))
+        product(3, quantize_vals(vt3_grouped, 3))
 
         out_codes = tile([P, Q], U32, "out_codes")
         out_scales = tile([P, Q], U8, "out_scales")
-        result_bf = [tile([P, P, PACK], BF16, f"result_bf{h}") for h in range(QT)]
-        nc.vector.tensor_copy(result_bf[0][:], o_banks[0][:].rearrange("p j q -> p q j"))
-        nc.scalar.copy(result_bf[1][:], o_banks[1][:].rearrange("p j q -> p q j"))
-        for h in range(QT):
-            quantize(out_codes[:, h * P : (h + 1) * P], out_scales[:, h * P : (h + 1) * P], result_bf[h][:].rearrange("p q j -> p (q j)"))
-        for h in (1, 0):
-            nc.scalar.copy(result[:, 3, h * P : (h + 1) * P], o_banks[h][:, 3, :])
+        out_grouped = [tile([P, P, PACK], BF16, f"out_grouped{h}") for h in range(HALVES)]
+        nc.vector.tensor_copy(out_grouped[0][:], o_banks[0][:].rearrange("p j q -> p q j"))
+        nc.scalar.copy(out_grouped[1][:], o_banks[1][:].rearrange("p j q -> p q j"))
+        for h in reversed(range(HALVES)):
+            quantize(out_codes[:, half(h)], out_scales[:, half(h)], out_grouped[h][:].rearrange("p q j -> p (q j)"))
+        last = PACK - 1
+        for h in reversed(range(HALVES)):
+            nc.scalar.copy(result[:, last, half(h)], o_banks[h][:, last, :])
         nc.sync.dma_start(out_1[0].rearrange("p q r -> p (q r)").bitcast(I32), out_codes[:].bitcast(I32))
-        for g in range(4):
+        for g in range(QUADRANTS):
             queue = (nc.sync, nc.scalar)[g % 2]
-            queue.dma_start(out_2[0, 4 * g : 4 * g + 4, :].bitcast(I32), out_scales[32 * g : 32 * g + 4, :].bitcast(I32))
-        nc.sync.dma_start(out_rows[:, 3, :], result[:, 3, :])
+            queue.dma_start(out_2[0, 4 * g : 4 * g + 4, :].bitcast(I32), out_scales[scale_rows(g), :].bitcast(I32))
+        nc.sync.dma_start(out_rows[:, last, :], result[:, last, :])

from contextlib import ExitStack

import concourse.mybir as mybir
from concourse.masks import make_identity

D, T, I, Q, E = 512, 2048, 512, 256, 512
P = 128
PACK = 4
HALVES = Q // P
QUADRANTS = 4
FLOPS = 2 * D * Q * I * 2 + 2 * I * E * Q

F32 = mybir.dt.float32
BF16 = mybir.dt.bfloat16
I32 = mybir.dt.int32
U32 = mybir.dt.uint32
U16 = mybir.dt.uint16
U8 = mybir.dt.uint8
FP8X4 = mybir.dt.float8_e4m3fn_x4
FP4X4 = mybir.dt.float4_e2m1fn_x4
ALU = mybir.AluOpType
ACT = mybir.ActivationFunctionType
AXIS = mybir.AxisListType


def tile_attend_antiquery_pl_kernel(tc, query, avoid, keys_words, keys_scales, aver, size, vals, offs, out_0, out_1, out_2):
    nc = tc.nc
    with ExitStack() as ctx:
        sbuf = ctx.enter_context(tc.tile_pool(name="sbuf", bufs=1))
        psum = ctx.enter_context(tc.psum_pool(name="psum", bufs=1))

        def tile(shape, dtype, name, reuse=None):
            return sbuf.tile(shape, dtype, name=name, tag=reuse or name, align_bytes=64)

        def bank(shape, tag, name):
            return psum.tile(shape, F32, tag=tag, name=name)

        def half(h):
            return slice(h * P, (h + 1) * P)

        def scale_rows(g):
            return slice(32 * g, 32 * g + 4)

        offsets = sbuf.tile([P, I // 16], U16, name="offsets")
        nc.sync.dma_start(offsets[:], offs)

        pool_scales = tile([P, T], U8, "pool_scales")
        nc.gpsimd.memset(pool_scales[:].bitcast(I32), 0)
        pool_words = tile([P, T], U16, "pool_words")
        nc.sync.dma_start(pool_words[:].bitcast(I32), keys_words[0].bitcast(I32))
        for g in range(QUADRANTS):
            nc.sync.dma_start(pool_scales[scale_rows(g), :].bitcast(I32), keys_scales[0, 4 * g : 4 * g + 4, :].bitcast(I32))
        avoid_raw = tile([P, PACK, Q], F32, "avoid_raw")
        nc.sync.dma_start(avoid_raw[:], avoid.rearrange("(p t) q -> p t q", t=PACK))
        query_raw = tile([P, PACK, Q], F32, "query_raw")
        nc.sync.dma_start(query_raw[:], query.rearrange("(p t) q -> p t q", t=PACK))

        vals_rows = vals.rearrange("(p j) c -> j p c", j=PACK)
        pool_vals = []

        def load_vals(j):
            window = tile([P, T], F32, f"pool_vals{j}")
            nc.sync.dma_start(window[:], vals_rows[j])
            pool_vals.append(window)

        load_vals(0)
        aver_cols = tile([P, HALVES], F32, "aver_cols")
        with nc.allow_non_contiguous_dma(reason="one value a partition"):
            nc.sync.dma_start(aver_cols[:], aver.rearrange("(h p) o -> p (h o)", p=P))
        size_cols = tile([P, PACK], F32, "size_cols")
        nc.sync.dma_start(size_cols[:], size.rearrange("o (p t) -> p (o t)", t=PACK))
        for j in range(1, PACK):
            load_vals(j)
        ident = tile([P, P], F32, "ident")
        make_identity(nc, ident[:])

        def group(engine_copy, grouped, raw):
            engine_copy(grouped.rearrange("p (c n) t -> p c t n", n=4), raw.rearrange("p t (c n) -> p c t n", n=4))

        def activation_copy(dst, src):
            nc.scalar.activation(dst, src, ACT.Copy)

        def quantize(codes, scales, grouped):
            nc.vector.quantize_mx(out=codes.bitcast(FP8X4), scales=scales, in_=grouped)

        avoid_grouped = tile([P, Q, PACK], BF16, "avoid_grouped")
        group(activation_copy, avoid_grouped[:], avoid_raw[:])
        key_words = tile([P, I], U16, "key_words")
        nc.vector.tensor_copy(key_words[:], pool_words[:].indirect(offsets[:]))
        key_scales = tile([P, I], U8, "key_scales")
        nc.vector.tensor_copy(key_scales[:], pool_scales[:].indirect(offsets[:]))
        query_grouped = [tile([P, P, PACK], BF16, f"query_grouped{h}") for h in range(HALVES)]
        group(nc.scalar.copy, query_grouped[0][:], query_raw[:, :, half(0)])
        group(nc.vector.tensor_copy, query_grouped[1][:], query_raw[:, :, half(1)])
        avoid_codes = tile([P, Q], U32, "avoid_codes")
        avoid_scales = tile([P, Q], U8, "avoid_scales")
        quantize(avoid_codes[:], avoid_scales[:], avoid_grouped[:].rearrange("p q t -> p (q t)"))

        def scores(dst, codes, scales):
            nc.tensor.matmul_mx(out=dst, lhsT=codes.bitcast(FP8X4), lhsT_scale=scales,
                                rhs=key_words[:].bitcast(FP4X4), rhs_scale=key_scales[:], start=True, stop=True)

        a_banks, b_banks = [], []
        for h in range(HALVES):
            b_bank = bank([P, I], f"b{h}", f"b_bank{h}")
            scores(b_bank[:], avoid_codes[:, half(h)], avoid_scales[:, half(h)])
            b_banks.append(b_bank)
            query_codes = tile([P, P], U32, f"query_codes{h}")
            query_scales = tile([P, P], U8, f"query_scales{h}")
            quantize(query_codes[:], query_scales[:], query_grouped[h][:].rearrange("p q t -> p (q t)"))
            a_bank = bank([P, I], f"a{h}", f"a_bank{h}")
            scores(a_bank[:], query_codes[:], query_scales[:])
            a_banks.append(a_bank)

        size_bank = bank([P, PACK, P], "size", "size_bank")
        for t in range(PACK):
            nc.tensor.transpose(size_bank[:, t, :], size_cols[:, t : t + 1].to_broadcast([P, P]), ident[:])

        neg_scores, probs = [], []
        for h in range(HALVES):
            positive = tile([P, I], F32, f"positive{h}")
            nc.scalar.activation(positive[:], b_banks[h][:], ACT.Relu)
            neg_s = tile([P, I], F32, f"neg_s{h}")
            nc.vector.scalar_tensor_tensor(neg_s[:], positive[:], aver_cols[:, h : h + 1], a_banks[h][:], ALU.mult, ALU.subtract)
            neg_scores.append(neg_s)
        totals = tile([P, HALVES], F32, "totals")
        for h in range(HALVES):
            neg_max = tile([P, 1], F32, f"neg_max{h}")
            nc.vector.tensor_reduce(neg_max[:], neg_scores[h][:], AXIS.X, ALU.min)
            prob = tile([P, I], F32, f"prob{h}")
            nc.scalar.activation(prob[:], neg_scores[h][:], ACT.Exp, bias=neg_max[:], scale=-1.0, accum_out=totals[:, h : h + 1])
            probs.append(prob)

        def turn(rows, tag, name, grouped):
            pairs = rows[:].bitcast(F32)
            turned = bank([P, 2, P], tag, name + "_bank")
            for u in range(2):
                nc.tensor.transpose(turned[:, u, :], pairs[:, u : 2 * P : 2], ident[:])
            nc.scalar.copy(grouped.bitcast(F32).rearrange("p (r u) -> p r u", u=2), turned[:].rearrange("p u r -> p r u"))

        def gather_vals(j):
            picked = tile([P, I], BF16, f"picked{j}")
            nc.vector.tensor_copy(picked[:], pool_vals[j][:].indirect(offsets[:]))
            grouped = tile([P, P * PACK], BF16, f"vt{j}_grouped")
            turn(picked, f"b{j % 2}", f"vt{j}", grouped[:])
            return grouped

        def weights(h):
            w = tile([P, I], BF16, f"w{h}")
            nc.vector.scalar_tensor_tensor(w[:].rearrange("p (n t) -> p n t", t=PACK), probs[h][:].rearrange("p (n t) -> p n t", t=PACK),
                                           inverses[:, h : h + 1], size_bank[:].rearrange("p t n -> p n t"), ALU.mult, ALU.mult)
            turn(w, f"w{h}", f"wt{h}", wt_grouped[:, h * I : (h + 1) * I])

        def quantize_vals(grouped, j, reuse=None):
            codes = tile([P, P], U32, f"vt{j}_codes", reuse)
            scales = tile([P, P], U8, f"vt{j}_scales")
            quantize(codes[:], scales[:], grouped[:])
            return codes, scales

        o_banks = [bank([P, PACK, P], f"a{h}", f"o_bank{h}") for h in range(HALVES)]
        result = tile([P, PACK, Q], F32, "result")
        out_rows = out_0.rearrange("(p j) q -> p j q", j=PACK)

        def product(j, vt):
            codes, scales = vt
            for h in range(HALVES):
                nc.tensor.matmul_mx(out=o_banks[h][:, j, :], lhsT=codes[:].bitcast(FP8X4), lhsT_scale=scales[:],
                                    rhs=wt_codes[:, half(h)].bitcast(FP8X4), rhs_scale=wt_scales[:, half(h)], start=True, stop=True)

        def unload(js, copies):
            for h in range(HALVES):
                copies[h](result[:, js, half(h)], o_banks[h][:, js, :])
            nc.sync.dma_start(out_rows[:, js, :], result[:, js, :])

        vt0_grouped = gather_vals(0)
        inverses = tile([P, HALVES], F32, "inverses")
        nc.vector.reciprocal(inverses[:], totals[:])
        wt_grouped = tile([P, HALVES * I], BF16, "wt_grouped")
        for h in range(HALVES):
            weights(h)
        vt1_grouped = gather_vals(1)
        vt0 = quantize_vals(vt0_grouped, 0)
        wt_codes = tile([P, Q], U32, "wt_codes")
        wt_scales = tile([P, Q], U8, "wt_scales")
        quantize(wt_codes[:], wt_scales[:], wt_grouped[:])
        product(0, vt0)
        vt2_grouped = gather_vals(2)
        product(1, quantize_vals(vt1_grouped, 1))
        unload(slice(0, 2), (nc.scalar.copy, nc.scalar.copy))
        vt3_grouped = gather_vals(3)
        product(2, quantize_vals(vt2_grouped, 2, reuse="pool_vals3"))
        unload(slice(2, 3), (nc.vector.tensor_copy, nc.scalar.copy))
        product(3, quantize_vals(vt3_grouped, 3))

        out_codes = tile([P, Q], U32, "out_codes")
        out_scales = tile([P, Q], U8, "out_scales")
        out_grouped = [tile([P, P, PACK], BF16, f"out_grouped{h}") for h in range(HALVES)]
        nc.vector.tensor_copy(out_grouped[0][:], o_banks[0][:].rearrange("p j q -> p q j"))
        nc.scalar.copy(out_grouped[1][:], o_banks[1][:].rearrange("p j q -> p q j"))
        for h in reversed(range(HALVES)):
            quantize(out_codes[:, half(h)], out_scales[:, half(h)], out_grouped[h][:].rearrange("p q j -> p (q j)"))
        last = PACK - 1
        for h in reversed(range(HALVES)):
            nc.scalar.copy(result[:, last, half(h)], o_banks[h][:, last, :])
        nc.sync.dma_start(out_1[0].rearrange("p q r -> p (q r)").bitcast(I32), out_codes[:].bitcast(I32))
        for g in range(QUADRANTS):
            queue = (nc.sync, nc.scalar)[g % 2]
            queue.dma_start(out_2[0, 4 * g : 4 * g + 4, :].bitcast(I32), out_scales[scale_rows(g), :].bitcast(I32))
        nc.sync.dma_start(out_rows[:, last, :], result[:, last, :])
